import numpy as np
import ml_dtypes


def mxq(x, axis, fmt="e4m3"):
    dtype, down = {"e4m3": (ml_dtypes.float8_e4m3fn, 7), "e5m2": (ml_dtypes.float8_e5m2, 14)}[fmt]
    v = np.moveaxis(np.asarray(x, np.float32).astype(ml_dtypes.bfloat16).astype(np.float64), axis, -1)
    blocks = v.reshape(v.shape[:-1] + (-1, 32))
    amax = np.abs(blocks).max(-1, keepdims=True)
    byte = np.maximum(np.where(amax > 0, np.frexp(amax)[1] - 1 + 127, 0) - down, 1)
    scale = np.exp2(byte - 127.0)
    codes = (blocks / scale).astype(np.float32).astype(dtype).astype(np.float64)
    return np.moveaxis((codes * scale).reshape(v.shape), -1, axis)


WIDE = False


def mx_kscale(k):
    if not WIDE:
        return np.ones(k)
    levels = np.array([10, -10, 5, -5, 0])
    if k % 512:
        return np.exp2(np.random.permutation(np.resize(levels, k // 32))).repeat(32)
    a = np.empty((k // 512, 16))
    for p in range(k // 512):
        a[p, :8] = np.random.permutation(np.resize(levels, 8))
        for g in range(8):
            far = levels[np.abs(levels - a[p, g]) >= 10]
            a[p, g + 8] = far[np.random.randint(len(far))]
    return np.exp2(a.ravel()).repeat(32)


def f64(x):
    return np.asarray(x).astype(np.float64)


def striped(idx):
    return np.tile(np.asarray(idx).reshape(-1, 16).T, (8, 1)).astype(np.uint16)


def unstriped(offs):
    return offs[:16].T.reshape(-1).astype(np.int64)


E2M1 = np.array([0.0, 0.5, 1.0, 1.5, 2.0, 3.0, 4.0, 6.0, -0.0, -0.5, -1.0, -1.5, -2.0, -3.0, -4.0, -6.0])


def pack_weight(w, fmt):
    k, n = w.shape
    w = f64(np.asarray(w, np.float32).astype(ml_dtypes.bfloat16)).reshape(k // 32, 32, n)
    amax = np.abs(w).max(1)
    if fmt == "e4m3":
        byte = np.frexp(amax)[1] - 1 + 127 - 7
    else:
        mant, ex = np.frexp(amax / 6.0)
        byte = np.where(mant > 0.5, ex, ex - 1) + 127
    byte = np.clip(np.where(amax > 0, byte, 1), 1, 254)
    scaled = (w * np.exp2(127.0 - byte)[:, None, :]).reshape(k, n).astype(np.float32)
    by_word = np.ascontiguousarray(scaled.reshape(k // 512, 128, 4, n).transpose(0, 1, 3, 2))
    if fmt == "e4m3":
        words = by_word.astype(ml_dtypes.float8_e4m3fn).view(np.uint8)
    else:
        c = by_word.astype(ml_dtypes.float4_e2m1fn).view(np.uint8) & 0xF
        words = (c[..., 0::2] | (c[..., 1::2] << 4)).reshape(k // 512, 128, 2 * n)
    return np.ascontiguousarray(words), np.ascontiguousarray(byte.astype(np.uint8).reshape(k // 512, 16, n))


def unpack_weight(words, scales, fmt):
    g, _, n = scales.shape
    words = np.ascontiguousarray(words).reshape(g, 128, n, -1)
    if fmt == "e4m3":
        vals = words.view(ml_dtypes.float8_e4m3fn).astype(np.float64)
    else:
        nib = np.empty((g, 128, n, 4), np.uint8)
        nib[..., 0::2] = words & 0xF
        nib[..., 1::2] = words >> 4
        vals = E2M1[nib]
    vals = vals * np.repeat(np.exp2(scales.astype(np.float64) - 127.0), 8, axis=1)[..., None]
    return vals.transpose(0, 1, 3, 2).reshape(g * 512, n)


K, R, F, T, J, M = 512, 128, 512, 2048, 512, 256


def setup_inputs():
    n = np.random.standard_normal
    idx = np.random.permutation(T)[:J]
    idx2 = np.random.permutation(J)[:M]
    idx3 = np.random.permutation(J)[:M]
    fk = mx_kscale(K)
    ff = mx_kscale(F)
    tabp = pack_weight(n((K, T)) / fk[:, None], "e2m1")
    dtabp = pack_weight(n((K, T)) / fk[:, None], "e2m1")
    return {
        "tab_words": tabp[0],
        "tab_scales": tabp[1],
        "w1": (n((K, R)) * 1 / np.sqrt(K) * fk[:, None]).astype(np.float32),
        "reserve": (np.random.uniform(0.3, 1.5, (R, 1))).astype(np.float32),
        "wo": (n((F, R)) * 1 / np.sqrt(F) * ff[:, None]).astype(np.float32),
        "dy": (n((F, M)) / ff[:, None]).astype(np.float32),
        "dtab_words": dtabp[0],
        "dtab_scales": dtabp[1],
        "og": (np.random.uniform(0.7, 2.0, (R, 1))).astype(np.float32),
        "base": (0.3 * n((R, J))).astype(np.float32),
        "offs": striped(idx),
        "offs2": striped(idx2),
        "offs3": striped(idx3),
    }


def reference(tab_words, tab_scales, w1, reserve, wo, dy, dtab_words, dtab_scales, og, base, offs, offs2, offs3):
    idx = unstriped(offs)
    idx2 = unstriped(offs2)
    idx3 = unstriped(offs3)
    tabu = unpack_weight(tab_words, tab_scales, "e2m1")
    dtabu = unpack_weight(dtab_words, dtab_scales, "e2m1")
    w1q = mxq(f64(w1), 0, "e4m3")
    tabidxg = tabu[:, idx]
    a = w1q.T @ tabidxg
    dtabidxg = dtabu[:, idx]
    ta = w1q.T @ dtabidxg
    h1 = np.exp(a)
    woq = mxq(f64(wo), 0, "e4m3")
    dyq = mxq(f64(dy), 0, "e4m3")
    c0 = woq.T @ dyq
    e1 = c0 / (h1[:, idx2] + h1[:, idx3] + f64(reserve))
    s1 = np.zeros((R, J))
    s1[:, idx2] = e1
    e2 = c0 * h1[:, idx2] / np.square(h1[:, idx2] + h1[:, idx3] + f64(reserve)) * (-1.0)
    s2 = np.zeros((R, J))
    s2[:, idx2] = e2
    e3 = c0 * h1[:, idx2] / np.square(h1[:, idx2] + h1[:, idx3] + f64(reserve)) * (-1.0)
    s3 = np.zeros((R, J))
    s3[:, idx3] = e3
    dh1 = s1 + s2 + s3
    xh1 = ta * h1
    xe1 = (xh1[:, idx2] + xh1[:, idx3]) * c0 / np.square(h1[:, idx2] + h1[:, idx3] + f64(reserve)) * (-1.0)
    xs1 = np.zeros((R, J))
    xs1[:, idx2] = xe1
    xe2 = (xh1[:, idx2] * c0 - (xh1[:, idx2] + xh1[:, idx3]) * (h1[:, idx2] + h1[:, idx3] + f64(reserve)) * 2.0 * c0 * h1[:, idx2] / np.square(h1[:, idx2] + h1[:, idx3] + f64(reserve))) / np.square(h1[:, idx2] + h1[:, idx3] + f64(reserve)) * (-1.0)
    xs2 = np.zeros((R, J))
    xs2[:, idx2] = xe2
    xe3 = (xh1[:, idx2] * c0 - (xh1[:, idx2] + xh1[:, idx3]) * (h1[:, idx2] + h1[:, idx3] + f64(reserve)) * 2.0 * c0 * h1[:, idx2] / np.square(h1[:, idx2] + h1[:, idx3] + f64(reserve))) / np.square(h1[:, idx2] + h1[:, idx3] + f64(reserve)) * (-1.0)
    xs3 = np.zeros((R, J))
    xs3[:, idx3] = xe3
    xdh1 = xs1 + xs2 + xs3
    xda = xdh1 * h1 + xh1 * dh1
    y = xda * f64(og) + f64(base)
    return y

@@ -1,0 +1,172 @@
+from contextlib import ExitStack
+
+import concourse.mybir as mybir
+from concourse.masks import make_identity
+
+K, R, F, T, J, M = 512, 128, 512, 2048, 512, 256
+FLOPS = 2 * K * R * J * 2 + 2 * F * R * M
+
+F32 = mybir.dt.float32
+BF16 = mybir.dt.bfloat16
+I32 = mybir.dt.int32
+U32 = mybir.dt.uint32
+U16 = mybir.dt.uint16
+U8 = mybir.dt.uint8
+FP8X4 = mybir.dt.float8_e4m3fn_x4
+FP4X4 = mybir.dt.float4_e2m1fn_x4
+ALU = mybir.AluOpType
+ACT = mybir.ActivationFunctionType
+
+P = 128
+PACK = 4
+QUADRANTS = 4
+ROWS = 4
+
+
+def tile_attend_hvratiopairs_kernel(tc, tab_words, tab_scales, w1, reserve, wo, dy, dtab_words, dtab_scales,
+                                     og, base, offs, offs2, offs3, out):
+    nc = tc.nc
+    with ExitStack() as ctx:
+        sb = ctx.enter_context(tc.tile_pool(name="sb", bufs=1))
+        ps = ctx.enter_context(tc.psum_pool(name="ps", bufs=1))
+
+        def tile(name, cols, dtype):
+            return sb.tile([P, cols], dtype, name=name, align_bytes=64)
+
+        list1 = tile("list1", J // 16, U16)
+        list2 = tile("list2", M // 16, U16)
+        list3 = tile("list3", M // 16, U16)
+        tab_w = tile("tab_w", T, U16)
+        dtab_w = tile("dtab_w", T, U16)
+        tab_s = tile("tab_s", T, U8)
+        dtab_s = tile("dtab_s", T, U8)
+        w1_raw = tile("w1_raw", PACK * R, F32)
+        wo_raw = tile("wo_raw", PACK * R, F32)
+        dy_raw = tile("dy_raw", PACK * M, F32)
+        base_sb = tile("base_sb", J, F32)
+        res = tile("res", 1, F32)
+        gain = tile("gain", 1, F32)
+        put2 = tile("put2", J, F32)
+        put3 = tile("put3", J, F32)
+
+        for window in (tab_s, dtab_s):
+            nc.vector.memset(window[:].bitcast(I32), 0)
+        nc.vector.memset(put2[:], 0.0)
+        nc.vector.memset(put3[:], 0.0)
+
+        def load_scales(dst, src):
+            for q in range(QUADRANTS):
+                nc.sync.dma_start(dst[32 * q:32 * q + ROWS, :].bitcast(I32),
+                                  src[0, ROWS * q:ROWS * (q + 1), :].bitcast(I32))
+
+        def load_rows(dst, src):
+            nc.sync.dma_start(dst[:], src.rearrange("(p t) w -> p (t w)", t=PACK))
+
+        nc.sync.dma_start(list1[:], offs)
+        nc.sync.dma_start(tab_w[:].bitcast(I32), tab_words[0].bitcast(I32))
+        load_scales(tab_s, tab_scales)
+        load_rows(w1_raw, w1)
+        nc.sync.dma_start(dtab_w[:].bitcast(I32), dtab_words[0].bitcast(I32))
+        load_rows(dy_raw, dy)
+        load_scales(dtab_s, dtab_scales)
+        load_rows(wo_raw, wo)
+        nc.sync.dma_start(list2[:], offs2)
+        nc.sync.dma_start(list3[:], offs3)
+        nc.sync.dma_start(base_sb[:], base)
+        nc.sync.dma_start(res[:], reserve)
+        nc.sync.dma_start(gain[:], og)
+        ident = tile("ident", P, F32)
+        make_identity(nc, ident[:])
+
+        def interleave(name, raw, width):
+            grouped = tile(name + "_bf16", PACK * width, BF16)
+            nc.scalar.copy(grouped[:].rearrange("p (w t) -> p w t", t=PACK),
+                           raw[:].rearrange("p (t w) -> p w t", t=PACK))
+            return grouped
+
+        def quantize(name, grouped, width):
+            codes = tile(name + "_codes", width, U32)
+            scales = tile(name + "_scales", width, U8)
+            nc.vector.quantize_mx(out=codes[:].bitcast(FP8X4), scales=scales[:], in_=grouped[:])
+            return codes, scales
+
+        def gather(name, window, offsets, n, dtype):
+            picked = tile(name, n, dtype)
+            nc.vector.tensor_copy(picked[:], window[:].indirect(offsets[:]))
+            return picked
+
+        def product(name, n, lhs, rhs_codes, rhs_scales):
+            bank = ps.tile([P, n], F32, name=name)
+            nc.tensor.matmul_mx(bank[:], lhsT=lhs[0][:].bitcast(FP8X4), lhsT_scale=lhs[1][:],
+                                rhs=rhs_codes, rhs_scale=rhs_scales, start=True, stop=True)
+            return bank
+
+        w1_g = interleave("w1", w1_raw, R)
+        tab_wg = gather("tab_wg", tab_w, list1, J, U16)
+        tab_sg = gather("tab_sg", tab_s, list1, J, U8)
+        w1_q = quantize("w1", w1_g, R)
+        a_ps = product("a_ps", J, w1_q, tab_wg[:].bitcast(FP4X4), tab_sg[:])
+        h1 = tile("h1", J, F32)
+        nc.scalar.activation(h1[:], a_ps[:], ACT.Exp)
+        dtab_wg = gather("dtab_wg", dtab_w, list1, J, U16)
+        dtab_sg = gather("dtab_sg", dtab_s, list1, J, U8)
+        ta_ps = product("ta_ps", J, w1_q, dtab_wg[:].bitcast(FP4X4), dtab_sg[:])
+        dy_g = interleave("dy", dy_raw, M)
+        wo_g = interleave("wo", wo_raw, R)
+        gain2 = tile("gain2", 1, F32)
+        nc.scalar.activation(gain2[:], gain[:], ACT.Copy, scale=2.0)
+
+        ha = gather("ha", h1, list2, M, F32)
+        xh1 = tile("xh1", J, F32)
+        nc.vector.tensor_tensor(xh1[:], ta_ps[:], h1[:], ALU.mult)
+        hsum = tile("hsum", M, F32)
+        nc.vector.tensor_tensor(hsum[:], h1[:].indirect(list3[:]), ha[:], ALU.add)
+        root = tile("root", M, F32)
+        nc.scalar.activation(root[:], hsum[:], ACT.Abs_reciprocal_sqrt, bias=res[:])
+        inv = tile("inv", M, F32)
+        nc.scalar.activation(inv[:], root[:], ACT.Square)
+        xa = gather("xa", xh1, list2, M, F32)
+        wo_q = quantize("wo", wo_g, R)
+        dy_q = quantize("dy", dy_g, M)
+        c_ps = product("c_ps", M, wo_q, dy_q[0][:].bitcast(FP8X4), dy_q[1][:])
+        xsum = tile("xsum", M, F32)
+        nc.vector.tensor_tensor(xsum[:], xh1[:].indirect(list3[:]), xa[:], ALU.add)
+
+        share = tile("share", M, F32)
+        nc.vector.tensor_tensor(share[:], ha[:], inv[:], ALU.mult)
+        cq = tile("cq", M, F32)
+        nc.vector.scalar_tensor_tensor(cq[:], c_ps[:], gain2[:], inv[:], ALU.mult, ALU.mult)
+        ps_x = tile("ps_x", M, F32)
+        nc.vector.tensor_tensor(ps_x[:], share[:], xsum[:], ALU.mult)
+        w = tile("w", M, F32)
+        nc.vector.tensor_tensor(w[:], ps_x[:], xa[:], ALU.subtract)
+        z = tile("z", M, F32)
+        nc.vector.scalar_tensor_tensor(z[:], xa[:], -0.5, ps_x[:], ALU.mult, ALU.add)
+        t2 = tile("t2", M, F32)
+        nc.vector.scalar_tensor_tensor(t2[:], share[:], -0.5, w[:], ALU.add, ALU.mult)
+        tr = tile("tr", M, F32)
+        nc.vector.scalar_tensor_tensor(tr[:], inv[:], res[:], z[:], ALU.mult, ALU.mult)
+        nc.vector.tensor_tensor(put2[:].indirect(list2[:]), cq[:], t2[:], ALU.mult)
+        t3 = tile("t3", M, F32)
+        nc.vector.tensor_tensor(t3[:], t2[:], tr[:], ALU.add)
+        half = J // 2
+        parts = []
+        for s in range(2):
+            turned_ps = ps.tile([P, half], F32, name="turned_ps%d" % s)
+            for b in range(half // P):
+                cols = slice(s * half + b * P, s * half + (b + 1) * P)
+                block = turned_ps[:, b * P:(b + 1) * P]
+                nc.tensor.matmul(block, base_sb[:, cols], ident[:], start=True, stop=False, is_transpose=True)
+                nc.tensor.matmul(block, put2[:, cols], ident[:], start=False, stop=True, is_transpose=True)
+            turned = tile("turned%d" % s, half, F32)
+            nc.scalar.copy(turned[:], turned_ps[:])
+            part = ps.tile([P, half], F32, name="part%d" % s)
+            for b in range(half // P):
+                nc.tensor.transpose(part[:, b * P:(b + 1) * P], turned[:, b * P:(b + 1) * P], ident[:])
+            parts.append(part)
+        nc.vector.tensor_tensor(put3[:].indirect(list3[:]), cq[:], t3[:], ALU.mult)
+        for s, queue in enumerate((nc.sync, nc.scalar)):
+            cols = slice(s * half, (s + 1) * half)
+            res_half = tile("y%d" % s, half, F32)
+            nc.vector.tensor_tensor(res_half[:], parts[s][:], put3[:, cols], ALU.subtract)
+            queue.dma_start(out[:, cols], res_half[:])

@@ -55,37 +55,36 @@ def tile_attend_hvratiopairs_kernel(tc, tab_words, tab_scales, w1, reserve, wo, 
         nc.vector.memset(put3[:], 0.0)
 
         def load_scales(dst, src):
-            for q in range(QUADRANTS):
-                nc.sync.dma_start(dst[32 * q:32 * q + ROWS, :].bitcast(I32),
-                                  src[0, ROWS * q:ROWS * (q + 1), :].bitcast(I32))
+            for i in range(ROWS):
+                nc.sync.dma_start(dst[i:P:32, :].bitcast(I32), src[0, i:QUADRANTS * ROWS:ROWS, :].bitcast(I32))
 
         def load_rows(dst, src):
             nc.sync.dma_start(dst[:], src.rearrange("(p t) w -> p (t w)", t=PACK))
 
         nc.sync.dma_start(list1[:], offs)
         nc.sync.dma_start(tab_w[:].bitcast(I32), tab_words[0].bitcast(I32))
-        load_scales(tab_s, tab_scales)
-        load_rows(w1_raw, w1)
-        nc.sync.dma_start(dtab_w[:].bitcast(I32), dtab_words[0].bitcast(I32))
-        load_rows(dy_raw, dy)
-        load_scales(dtab_s, dtab_scales)
-        load_rows(wo_raw, wo)
         nc.sync.dma_start(list2[:], offs2)
         nc.sync.dma_start(list3[:], offs3)
-        nc.sync.dma_start(base_sb[:], base)
+        load_scales(tab_s, tab_scales)
+        load_rows(w1_raw, w1)
+        load_scales(dtab_s, dtab_scales)
+        nc.sync.dma_start(dtab_w[:].bitcast(I32), dtab_words[0].bitcast(I32))
+        load_rows(wo_raw, wo)
+        load_rows(dy_raw, dy)
         nc.sync.dma_start(res[:], reserve)
         nc.sync.dma_start(gain[:], og)
+        nc.sync.dma_start(base_sb[:], base)
         ident = tile("ident", P, F32)
         make_identity(nc, ident[:])
 
         def interleave(name, raw, width):
             grouped = tile(name + "_bf16", PACK * width, BF16)
-            nc.scalar.copy(grouped[:].rearrange("p (w t) -> p w t", t=PACK),
-                           raw[:].rearrange("p (t w) -> p w t", t=PACK))
+            nc.scalar.copy(grouped[:].rearrange("p (c i t) -> p c t i", t=PACK, i=4),
+                           raw[:].rearrange("p (t c i) -> p c t i", t=PACK, i=4))
             return grouped
 
-        def quantize(name, grouped, width):
-            codes = tile(name + "_codes", width, U32)
+        def quantize(name, grouped, width, codes_name=None):
+            codes = tile(codes_name or name + "_codes", width, U32)
             scales = tile(name + "_scales", width, U8)
             nc.vector.quantize_mx(out=codes[:].bitcast(FP8X4), scales=scales[:], in_=grouped[:])
             return codes, scales
@@ -108,18 +107,25 @@ def tile_attend_hvratiopairs_kernel(tc, tab_words, tab_scales, w1, reserve, wo, 
         a_ps = product("a_ps", J, w1_q, tab_wg[:].bitcast(FP4X4), tab_sg[:])
         h1 = tile("h1", J, F32)
         nc.scalar.activation(h1[:], a_ps[:], ACT.Exp)
-        dtab_wg = gather("dtab_wg", dtab_w, list1, J, U16)
+        warm = tile("dy_bf16", 1, F32)
+        nc.scalar.activation(warm[:], h1[:, 0:1], ACT.Abs_reciprocal_sqrt)
         dtab_sg = gather("dtab_sg", dtab_s, list1, J, U8)
-        ta_ps = product("ta_ps", J, w1_q, dtab_wg[:].bitcast(FP4X4), dtab_sg[:])
-        dy_g = interleave("dy", dy_raw, M)
+        ta_ps = ps.tile([P, J], F32, name="ta_ps")
+        for s in range(2):
+            cols = slice(s * M, (s + 1) * M)
+            dtab_wg = tile("dtab_wg%d" % s, M, U16)
+            nc.vector.tensor_copy(dtab_wg[:], dtab_w[:].indirect(list1[:, s * M // 16:(s + 1) * M // 16]))
+            nc.tensor.matmul_mx(ta_ps[:, cols], lhsT=w1_q[0][:].bitcast(FP8X4), lhsT_scale=w1_q[1][:],
+                                rhs=dtab_wg[:].bitcast(FP4X4), rhs_scale=dtab_sg[:, cols], start=True, stop=True)
         wo_g = interleave("wo", wo_raw, R)
+        dy_g = interleave("dy", dy_raw, M)
         gain2 = tile("gain2", 1, F32)
         nc.scalar.activation(gain2[:], gain[:], ACT.Copy, scale=2.0)
 
-        ha = gather("ha", h1, list2, M, F32)
+        ha = gather("dtab_w", h1, list2, M, F32)
         xh1 = tile("xh1", J, F32)
         nc.vector.tensor_tensor(xh1[:], ta_ps[:], h1[:], ALU.mult)
-        hsum = tile("hsum", M, F32)
+        hsum = tile("dtab_wg1", M, F32)
         nc.vector.tensor_tensor(hsum[:], h1[:].indirect(list3[:]), ha[:], ALU.add)
         root = tile("root", M, F32)
         nc.scalar.activation(root[:], hsum[:], ACT.Abs_reciprocal_sqrt, bias=res[:])
@@ -127,7 +133,7 @@ def tile_attend_hvratiopairs_kernel(tc, tab_words, tab_scales, w1, reserve, wo, 
         nc.scalar.activation(inv[:], root[:], ACT.Square)
         xa = gather("xa", xh1, list2, M, F32)
         wo_q = quantize("wo", wo_g, R)
-        dy_q = quantize("dy", dy_g, M)
+        dy_q = quantize("dy", dy_g, M, "h1")
         c_ps = product("c_ps", M, wo_q, dy_q[0][:].bitcast(FP8X4), dy_q[1][:])
         xsum = tile("xsum", M, F32)
         nc.vector.tensor_tensor(xsum[:], xh1[:].indirect(list3[:]), xa[:], ALU.add)
@@ -146,24 +152,27 @@ def tile_attend_hvratiopairs_kernel(tc, tab_words, tab_scales, w1, reserve, wo, 
         nc.vector.scalar_tensor_tensor(t2[:], share[:], -0.5, w[:], ALU.add, ALU.mult)
         tr = tile("tr", M, F32)
         nc.vector.scalar_tensor_tensor(tr[:], inv[:], res[:], z[:], ALU.mult, ALU.mult)
+        turned_ps = []
+        for b in range(J // P):
+            bank = ps.tile([P, P], F32, name="turned_ps%d" % b)
+            nc.tensor.matmul(bank[:], base_sb[:, b * P:(b + 1) * P], ident[:], start=True, stop=False,
+                             is_transpose=True)
+            turned_ps.append(bank)
         nc.vector.tensor_tensor(put2[:].indirect(list2[:]), cq[:], t2[:], ALU.mult)
         t3 = tile("t3", M, F32)
         nc.vector.tensor_tensor(t3[:], t2[:], tr[:], ALU.add)
         half = J // 2
-        parts = []
-        for s in range(2):
-            turned_ps = ps.tile([P, half], F32, name="turned_ps%d" % s)
-            for b in range(half // P):
-                cols = slice(s * half + b * P, s * half + (b + 1) * P)
-                block = turned_ps[:, b * P:(b + 1) * P]
-                nc.tensor.matmul(block, base_sb[:, cols], ident[:], start=True, stop=False, is_transpose=True)
-                nc.tensor.matmul(block, put2[:, cols], ident[:], start=False, stop=True, is_transpose=True)
-            turned = tile("turned%d" % s, half, F32)
-            nc.scalar.copy(turned[:], turned_ps[:])
-            part = ps.tile([P, half], F32, name="part%d" % s)
-            for b in range(half // P):
-                nc.tensor.transpose(part[:, b * P:(b + 1) * P], turned[:, b * P:(b + 1) * P], ident[:])
-            parts.append(part)
+        turned = []
+        for b in range(J // P):
+            nc.tensor.matmul(turned_ps[b][:], put2[:, b * P:(b + 1) * P], ident[:], start=False, stop=True,
+                             is_transpose=True)
+            block = tile("turned%d" % b, P, F32)
+            nc.scalar.copy(block[:], turned_ps[b][:])
+            turned.append(block)
+        parts = [ps.tile([P, half], F32, name=name) for name in ("a_ps", "ta_ps")]
+        for b in range(J // P):
+            s, c = divmod(b * P, half)
+            nc.tensor.transpose(parts[s][:, c:c + P], turned[b][:], ident[:])
         nc.vector.tensor_tensor(put3[:].indirect(list3[:]), cq[:], t3[:], ALU.mult)
         for s, queue in enumerate((nc.sync, nc.scalar)):
             cols = slice(s * half, (s + 1) * half)

@@ -1,7 +1,6 @@
 from contextlib import ExitStack
 
 import concourse.mybir as mybir
-from concourse.masks import make_identity
 
 K, R, F, T, J, M = 512, 128, 512, 2048, 512, 256
 FLOPS = 2 * K * R * J * 2 + 2 * F * R * M
@@ -74,8 +73,6 @@ def tile_attend_hvratiopairs_kernel(tc, tab_words, tab_scales, w1, reserve, wo, 
         nc.sync.dma_start(res[:], reserve)
         nc.sync.dma_start(gain[:], og)
         nc.sync.dma_start(base_sb[:], base)
-        ident = tile("ident", P, F32)
-        make_identity(nc, ident[:])
 
         def interleave(name, raw, width):
             grouped = tile(name + "_bf16", PACK * width, BF16)
@@ -119,8 +116,6 @@ def tile_attend_hvratiopairs_kernel(tc, tab_words, tab_scales, w1, reserve, wo, 
                                 rhs=dtab_wg[:].bitcast(FP4X4), rhs_scale=dtab_sg[:, cols], start=True, stop=True)
         wo_g = interleave("wo", wo_raw, R)
         dy_g = interleave("dy", dy_raw, M)
-        gain2 = tile("gain2", 1, F32)
-        nc.scalar.activation(gain2[:], gain[:], ACT.Copy, scale=2.0)
 
         ha = gather("dtab_w", h1, list2, M, F32)
         xh1 = tile("xh1", J, F32)
@@ -138,44 +133,33 @@ def tile_attend_hvratiopairs_kernel(tc, tab_words, tab_scales, w1, reserve, wo, 
         xsum = tile("xsum", M, F32)
         nc.vector.tensor_tensor(xsum[:], xh1[:].indirect(list3[:]), xa[:], ALU.add)
 
-        share = tile("share", M, F32)
-        nc.vector.tensor_tensor(share[:], ha[:], inv[:], ALU.mult)
+        share2 = tile("share2", M, F32)
+        nc.vector.scalar_tensor_tensor(share2[:], ha[:], 2.0, inv[:], ALU.mult, ALU.mult)
         cq = tile("cq", M, F32)
-        nc.vector.scalar_tensor_tensor(cq[:], c_ps[:], gain2[:], inv[:], ALU.mult, ALU.mult)
-        ps_x = tile("ps_x", M, F32)
-        nc.vector.tensor_tensor(ps_x[:], share[:], xsum[:], ALU.mult)
+        nc.vector.scalar_tensor_tensor(cq[:], c_ps[:], gain[:], inv[:], ALU.mult, ALU.mult)
+        px2 = tile("px2", M, F32)
+        nc.vector.tensor_tensor(px2[:], share2[:], xsum[:], ALU.mult)
+        k2 = tile("k2", M, F32)
+        nc.vector.scalar_tensor_tensor(k2[:], share2[:], -1.0, cq[:], ALU.add, ALU.mult)
         w = tile("w", M, F32)
-        nc.vector.tensor_tensor(w[:], ps_x[:], xa[:], ALU.subtract)
+        nc.vector.scalar_tensor_tensor(w[:], px2[:], 0.5, xa[:], ALU.mult, ALU.subtract)
+        kr = tile("kr", M, F32)
+        nc.vector.scalar_tensor_tensor(kr[:], inv[:], res[:], cq[:], ALU.mult, ALU.mult)
+        v2 = tile("v2", M, F32)
+        nc.vector.tensor_tensor(v2[:], k2[:], w[:], ALU.mult)
         z = tile("z", M, F32)
-        nc.vector.scalar_tensor_tensor(z[:], xa[:], -0.5, ps_x[:], ALU.mult, ALU.add)
-        t2 = tile("t2", M, F32)
-        nc.vector.scalar_tensor_tensor(t2[:], share[:], -0.5, w[:], ALU.add, ALU.mult)
-        tr = tile("tr", M, F32)
-        nc.vector.scalar_tensor_tensor(tr[:], inv[:], res[:], z[:], ALU.mult, ALU.mult)
-        turned_ps = []
-        for b in range(J // P):
-            bank = ps.tile([P, P], F32, name="turned_ps%d" % b)
-            nc.tensor.matmul(bank[:], base_sb[:, b * P:(b + 1) * P], ident[:], start=True, stop=False,
-                             is_transpose=True)
-            turned_ps.append(bank)
-        nc.vector.tensor_tensor(put2[:].indirect(list2[:]), cq[:], t2[:], ALU.mult)
-        t3 = tile("t3", M, F32)
-        nc.vector.tensor_tensor(t3[:], t2[:], tr[:], ALU.add)
+        nc.vector.tensor_tensor(z[:], px2[:], xa[:], ALU.subtract)
+        nc.vector.tensor_copy(put2[:].indirect(list2[:]), v2[:])
+        vr = tile("vr", M, F32)
+        nc.gpsimd.tensor_tensor(vr[:], kr[:], z[:], ALU.mult)
+        v3 = tile("v3", M, F32)
+        nc.gpsimd.tensor_tensor(v3[:], vr[:], v2[:], ALU.add)
+        nc.vector.tensor_copy(put3[:].indirect(list3[:]), v3[:])
+        part = tile("part", J, F32)
+        nc.gpsimd.tensor_tensor(part[:], put2[:], base_sb[:], ALU.add)
         half = J // 2
-        turned = []
-        for b in range(J // P):
-            nc.tensor.matmul(turned_ps[b][:], put2[:, b * P:(b + 1) * P], ident[:], start=False, stop=True,
-                             is_transpose=True)
-            block = tile("turned%d" % b, P, F32)
-            nc.scalar.copy(block[:], turned_ps[b][:])
-            turned.append(block)
-        parts = [ps.tile([P, half], F32, name=name) for name in ("a_ps", "ta_ps")]
-        for b in range(J // P):
-            s, c = divmod(b * P, half)
-            nc.tensor.transpose(parts[s][:, c:c + P], turned[b][:], ident[:])
-        nc.vector.tensor_tensor(put3[:].indirect(list3[:]), cq[:], t3[:], ALU.mult)
         for s, queue in enumerate((nc.sync, nc.scalar)):
             cols = slice(s * half, (s + 1) * half)
             res_half = tile("y%d" % s, half, F32)
-            nc.vector.tensor_tensor(res_half[:], parts[s][:], put3[:, cols], ALU.subtract)
+            nc.vector.tensor_tensor(res_half[:], part[:, cols], put3[:, cols], ALU.subtract)
             queue.dma_start(out[:, cols], res_half[:])

@@ -145,17 +145,17 @@ def tile_attend_hvratiopairs_kernel(tc, tab_words, tab_scales, w1, reserve, wo, 
         nc.vector.scalar_tensor_tensor(w[:], px2[:], 0.5, xa[:], ALU.mult, ALU.subtract)
         kr = tile("kr", M, F32)
         nc.vector.scalar_tensor_tensor(kr[:], inv[:], res[:], cq[:], ALU.mult, ALU.mult)
-        v2 = tile("v2", M, F32)
-        nc.vector.tensor_tensor(v2[:], k2[:], w[:], ALU.mult)
         z = tile("z", M, F32)
         nc.vector.tensor_tensor(z[:], px2[:], xa[:], ALU.subtract)
-        nc.vector.tensor_copy(put2[:].indirect(list2[:]), v2[:])
+        v2 = tile("v2", M, F32)
+        nc.vector.tensor_tensor(v2[:], k2[:], w[:], ALU.mult)
         vr = tile("vr", M, F32)
-        nc.gpsimd.tensor_tensor(vr[:], kr[:], z[:], ALU.mult)
+        nc.vector.tensor_tensor(vr[:], kr[:], z[:], ALU.mult)
+        nc.vector.tensor_copy(put2[:].indirect(list2[:]), v2[:])
         v3 = tile("v3", M, F32)
         nc.gpsimd.tensor_tensor(v3[:], vr[:], v2[:], ALU.add)
         nc.vector.tensor_copy(put3[:].indirect(list3[:]), v3[:])
-        part = tile("part", J, F32)
+        part = tile("vr", J, F32)
         nc.gpsimd.tensor_tensor(part[:], put2[:], base_sb[:], ALU.add)
         half = J // 2
         for s, queue in enumerate((nc.sync, nc.scalar)):

from contextlib import ExitStack

import concourse.mybir as mybir

K, R, F, T, J, M = 512, 128, 512, 2048, 512, 256
FLOPS = 2 * K * R * J * 2 + 2 * F * R * M

F32 = mybir.dt.float32
BF16 = mybir.dt.bfloat16
I32 = mybir.dt.int32
U32 = mybir.dt.uint32
U16 = mybir.dt.uint16
U8 = mybir.dt.uint8
FP8X4 = mybir.dt.float8_e4m3fn_x4
FP4X4 = mybir.dt.float4_e2m1fn_x4
ALU = mybir.AluOpType
ACT = mybir.ActivationFunctionType

P = 128
PACK = 4
QUADRANTS = 4
ROWS = 4


def tile_attend_hvratiopairs_kernel(tc, tab_words, tab_scales, w1, reserve, wo, dy, dtab_words, dtab_scales,
                                     og, base, offs, offs2, offs3, out):
    nc = tc.nc
    with ExitStack() as ctx:
        sb = ctx.enter_context(tc.tile_pool(name="sb", bufs=1))
        ps = ctx.enter_context(tc.psum_pool(name="ps", bufs=1))

        def tile(name, cols, dtype):
            return sb.tile([P, cols], dtype, name=name, align_bytes=64)

        list1 = tile("list1", J // 16, U16)
        list2 = tile("list2", M // 16, U16)
        list3 = tile("list3", M // 16, U16)
        tab_w = tile("tab_w", T, U16)
        dtab_w = tile("dtab_w", T, U16)
        tab_s = tile("tab_s", T, U8)
        dtab_s = tile("dtab_s", T, U8)
        w1_raw = tile("w1_raw", PACK * R, F32)
        wo_raw = tile("wo_raw", PACK * R, F32)
        dy_raw = tile("dy_raw", PACK * M, F32)
        base_sb = tile("base_sb", J, F32)
        res = tile("res", 1, F32)
        gain = tile("gain", 1, F32)
        put2 = tile("put2", J, F32)
        put3 = tile("put3", J, F32)

        for window in (tab_s, dtab_s):
            nc.vector.memset(window[:].bitcast(I32), 0)
        nc.vector.memset(put2[:], 0.0)
        nc.vector.memset(put3[:], 0.0)

        def load_scales(dst, src):
            for i in range(ROWS):
                nc.sync.dma_start(dst[i:P:32, :].bitcast(I32), src[0, i:QUADRANTS * ROWS:ROWS, :].bitcast(I32))

        def load_rows(dst, src):
            nc.sync.dma_start(dst[:], src.rearrange("(p t) w -> p (t w)", t=PACK))

        nc.sync.dma_start(list1[:], offs)
        nc.sync.dma_start(tab_w[:].bitcast(I32), tab_words[0].bitcast(I32))
        nc.sync.dma_start(list2[:], offs2)
        nc.sync.dma_start(list3[:], offs3)
        load_scales(tab_s, tab_scales)
        load_rows(w1_raw, w1)
        load_scales(dtab_s, dtab_scales)
        nc.sync.dma_start(dtab_w[:].bitcast(I32), dtab_words[0].bitcast(I32))
        load_rows(wo_raw, wo)
        load_rows(dy_raw, dy)
        nc.sync.dma_start(res[:], reserve)
        nc.sync.dma_start(gain[:], og)
        nc.sync.dma_start(base_sb[:], base)

        def interleave(name, raw, width):
            grouped = tile(name + "_bf16", PACK * width, BF16)
            nc.scalar.copy(grouped[:].rearrange("p (c i t) -> p c t i", t=PACK, i=4),
                           raw[:].rearrange("p (t c i) -> p c t i", t=PACK, i=4))
            return grouped

        def quantize(name, grouped, width, codes_name=None):
            codes = tile(codes_name or name + "_codes", width, U32)
            scales = tile(name + "_scales", width, U8)
            nc.vector.quantize_mx(out=codes[:].bitcast(FP8X4), scales=scales[:], in_=grouped[:])
            return codes, scales

        def gather(name, window, offsets, n, dtype):
            picked = tile(name, n, dtype)
            nc.vector.tensor_copy(picked[:], window[:].indirect(offsets[:]))
            return picked

        def product(name, n, lhs, rhs_codes, rhs_scales):
            bank = ps.tile([P, n], F32, name=name)
            nc.tensor.matmul_mx(bank[:], lhsT=lhs[0][:].bitcast(FP8X4), lhsT_scale=lhs[1][:],
                                rhs=rhs_codes, rhs_scale=rhs_scales, start=True, stop=True)
            return bank

        w1_g = interleave("w1", w1_raw, R)
        tab_wg = gather("tab_wg", tab_w, list1, J, U16)
        tab_sg = gather("tab_sg", tab_s, list1, J, U8)
        w1_q = quantize("w1", w1_g, R)
        a_ps = product("a_ps", J, w1_q, tab_wg[:].bitcast(FP4X4), tab_sg[:])
        h1 = tile("h1", J, F32)
        nc.scalar.activation(h1[:], a_ps[:], ACT.Exp)
        warm = tile("dy_bf16", 1, F32)
        nc.scalar.activation(warm[:], h1[:, 0:1], ACT.Abs_reciprocal_sqrt)
        dtab_sg = gather("dtab_sg", dtab_s, list1, J, U8)
        ta_ps = ps.tile([P, J], F32, name="ta_ps")
        for s in range(2):
            cols = slice(s * M, (s + 1) * M)
            dtab_wg = tile("dtab_wg%d" % s, M, U16)
            nc.vector.tensor_copy(dtab_wg[:], dtab_w[:].indirect(list1[:, s * M // 16:(s + 1) * M // 16]))
            nc.tensor.matmul_mx(ta_ps[:, cols], lhsT=w1_q[0][:].bitcast(FP8X4), lhsT_scale=w1_q[1][:],
                                rhs=dtab_wg[:].bitcast(FP4X4), rhs_scale=dtab_sg[:, cols], start=True, stop=True)
        wo_g = interleave("wo", wo_raw, R)
        dy_g = interleave("dy", dy_raw, M)

        ha = gather("dtab_w", h1, list2, M, F32)
        xh1 = tile("xh1", J, F32)
        nc.vector.tensor_tensor(xh1[:], ta_ps[:], h1[:], ALU.mult)
        hsum = tile("dtab_wg1", M, F32)
        nc.vector.tensor_tensor(hsum[:], h1[:].indirect(list3[:]), ha[:], ALU.add)
        root = tile("root", M, F32)
        nc.scalar.activation(root[:], hsum[:], ACT.Abs_reciprocal_sqrt, bias=res[:])
        inv = tile("inv", M, F32)
        nc.scalar.activation(inv[:], root[:], ACT.Square)
        xa = gather("xa", xh1, list2, M, F32)
        wo_q = quantize("wo", wo_g, R)
        dy_q = quantize("dy", dy_g, M, "h1")
        c_ps = product("c_ps", M, wo_q, dy_q[0][:].bitcast(FP8X4), dy_q[1][:])
        xsum = tile("xsum", M, F32)
        nc.vector.tensor_tensor(xsum[:], xh1[:].indirect(list3[:]), xa[:], ALU.add)

        share2 = tile("share2", M, F32)
        nc.vector.scalar_tensor_tensor(share2[:], ha[:], 2.0, inv[:], ALU.mult, ALU.mult)
        cq = tile("cq", M, F32)
        nc.vector.scalar_tensor_tensor(cq[:], c_ps[:], gain[:], inv[:], ALU.mult, ALU.mult)
        px2 = tile("px2", M, F32)
        nc.vector.tensor_tensor(px2[:], share2[:], xsum[:], ALU.mult)
        k2 = tile("k2", M, F32)
        nc.vector.scalar_tensor_tensor(k2[:], share2[:], -1.0, cq[:], ALU.add, ALU.mult)
        w = tile("w", M, F32)
        nc.vector.scalar_tensor_tensor(w[:], px2[:], 0.5, xa[:], ALU.mult, ALU.subtract)
        kr = tile("kr", M, F32)
        nc.vector.scalar_tensor_tensor(kr[:], inv[:], res[:], cq[:], ALU.mult, ALU.mult)
        z = tile("z", M, F32)
        nc.vector.tensor_tensor(z[:], px2[:], xa[:], ALU.subtract)
        v2 = tile("v2", M, F32)
        nc.vector.tensor_tensor(v2[:], k2[:], w[:], ALU.mult)
        vr = tile("vr", M, F32)
        nc.vector.tensor_tensor(vr[:], kr[:], z[:], ALU.mult)
        nc.vector.tensor_copy(put2[:].indirect(list2[:]), v2[:])
        v3 = tile("v3", M, F32)
        nc.gpsimd.tensor_tensor(v3[:], vr[:], v2[:], ALU.add)
        nc.vector.tensor_copy(put3[:].indirect(list3[:]), v3[:])
        part = tile("vr", J, F32)
        nc.gpsimd.tensor_tensor(part[:], put2[:], base_sb[:], ALU.add)
        half = J // 2
        for s, queue in enumerate((nc.sync, nc.scalar)):
            cols = slice(s * half, (s + 1) * half)
            res_half = tile("y%d" % s, half, F32)
            nc.vector.tensor_tensor(res_half[:], part[:, cols], put3[:, cols], ALU.subtract)
            queue.dma_start(out[:, cols], res_half[:])
